import numpy as np, ml_dtypes
CORES = [88,96,104,112,120,216,224,232,240,248]
N = 10
W = 64
def setup_inputs(rng):
    return {"x": rng.standard_normal((N, 128, W), dtype=np.float32).astype(ml_dtypes.bfloat16), "a": (7 + rng.standard_normal((N, 128, W), dtype=np.float32) - 9 * (rng.random((N, 128, W)) < 2.0 / (N * W))).astype(ml_dtypes.bfloat16)}
def setup_inputs_big(rng):
    d = setup_inputs(rng)
    for k in ("x",): d[k] = (d[k].astype(np.float32) * 1048576.0).astype(d[k].dtype)
    return d
def setup_inputs_small(rng):
    d = setup_inputs(rng)
    for k in ("x",): d[k] = (d[k].astype(np.float32) * (1 / 1048576.0)).astype(d[k].dtype)
    return d
def setup_inputs_apart(rng):
    d = setup_inputs(rng)
    f = (10.0 ** rng.permutation(np.linspace(-1.5, 1.5, N))).astype(np.float32).reshape(N, 1, 1)
    for k in ("x",): d[k] = (d[k].astype(np.float32) * f).astype(d[k].dtype)
    return d
def reference(x, a):
    X = np.concatenate(list(x.astype(np.float64)), axis=1); G = 1.0 / (1.0 + np.exp(-np.concatenate(list(a.astype(np.float64)), axis=1)))
    h = np.zeros(128); H = np.zeros_like(X)
    for c in range(N * W):
        h = G[:, c] * h + X[:, c]; H[:, c] = h
    return {"y": np.stack([H[:, W * r:W * r + W] for r in range(N)]).astype(ml_dtypes.bfloat16)}

@@ -1,0 +1,117 @@
+from concourse.bass import DstId, RemoteDMATransfer
+from concourse.mybir import AluOpType, AxisListType, ActivationFunctionType
+
+N = 10
+W = 64
+SIM_CORES = 256
+HOP1_ENGINES = 8
+DESTS_PER_ENGINE = 3
+
+SCRATCH = {
+    "a_sb": ("sbuf", [128, W], "bfloat16"),
+    "x_sb": ("sbuf", [128, W], "bfloat16"),
+    "gate": ("sbuf", [128, W], "float32"),
+    "loc": ("sbuf", [128, W + 1], "float32"),
+    "stage": ("dram", [128, 2], "float32"),
+    "land": ("dram", [N - 1, 128, 2], "float32"),
+    "rows": ("sbuf", [128, 256], "float32"),
+    "ones": ("sbuf", [128, N - 1], "float32"),
+    "ident": ("sbuf", [128, N - 1], "float32"),
+    "ps_s": ("psum", [128, 512], "float32"),
+    "ps_p": ("psum", [128, 512], "float32"),
+    "s_sb": ("sbuf", [128, N - 1], "float32"),
+    "car": ("sbuf", [128, N - 1], "float32"),
+    "y_sb": ("sbuf", [128, W], "bfloat16"),
+}
+SEMAPHORES = ["la", "lx", "on", "idn", "sg", "sv", "arr", "sent", "lr", "m1", "m2", "cp", "cc", "sy", "st"]
+
+
+def _bits(mask):
+    return [1 << b for b in range(mask.bit_length()) if (mask >> b) & 1]
+
+
+def _port_owner(c, dests, topo):
+    ok = [d for d in range(SIM_CORES)
+          if d != c and topo.host(d) == topo.host(c) and topo.chip(d) == topo.chip(c)
+          and all(topo.may_write(d, k) for k in dests)]
+    same = [d for d in ok if topo.die(d) == topo.die(c)]
+    return (same or ok)[0]
+
+
+def _relay_program(g, core, j, T, topo):
+    sem = T.sem
+    dests = list(T.cores[j + 1:])
+    common = topo.mask(core, dests[0])
+    for d in dests:
+        common &= topo.mask(core, d)
+    engines = _bits(common)[0::2]
+    transfers = []
+    for i in range(0, len(dests), DESTS_PER_ENGINE):
+        part = dests[i:i + DESTS_PER_ENGINE]
+        ids = []
+        for d in part:
+            rid, pid = topo.addr(d, core)
+            ids.append(DstId(rid=rid, pnc=pid))
+        transfers.append(RemoteDMATransfer(dst_ids=ids, dma_engine_mask=engines[len(transfers)], remote_sem=sem.arr,
+                                           srcs=[T.stage[:]], dsts=[T.land[j] for _ in part]))
+    g.wait_ge(sem.arr, HOP1_ENGINES)
+    g.remote_dma_fused(transfers, local_sem=sem.sent)
+    g.wait_ge(sem.sent, len(transfers))
+
+
+def rank_program(g, core, T, topo):
+    sem = T.sem
+    mult, add = AluOpType.mult, AluOpType.add
+    r = T.rank_of(core)
+    if r is None:
+        for j in range(N - 1):
+            if _port_owner(T.cores[j], T.cores[j + 1:], topo) == core:
+                _relay_program(g, core, j, T, topo)
+        return
+
+    g.sync.dma_start(T.a_sb[:], T.a[:]).then_inc(sem.la, 16)
+    g.sync.dma_start(T.x_sb[:], T.x[:]).then_inc(sem.lx, 16)
+
+    if r > 0:
+        g.vector.memset(T.ones[0:r, 0:r], 1.0).then_inc(sem.on, 1)
+        g.wait_ge(sem.on, 1)
+        g.affine_select(T.ident[0:r, 0:r], T.ones[0:r, 0:r], [[-1, r]], AluOpType.is_equal, 0.0, 0, 1).then_inc(sem.idn, 1)
+
+    g.scalar.wait_ge(sem.la, 16)
+    g.scalar.activation(T.gate[:], T.a_sb[:], ActivationFunctionType.Sigmoid).then_inc(sem.sg, 1)
+
+    g.vector.wait_ge(sem.sg, 1)
+    if r < N - 1:
+        g.vector.tensor_reduce(T.loc[:, W:W + 1], T.gate[:], AxisListType.X, mult).then_inc(sem.sv, 1)
+        g.vector.wait_ge(sem.lx, 16)
+        g.vector.tensor_tensor_scan(T.loc[:, 0:W], T.gate[:], T.x_sb[:], 0.0, mult, add).then_inc(sem.sv, 1)
+        relay = _port_owner(core, T.cores[r + 1:], topo)
+        rid, pid = topo.addr(relay, core)
+        m = sum(_bits(topo.mask(core, relay))[:HOP1_ENGINES])
+        g.wait_ge(sem.sv, 2)
+        g.remote_dma(T.stage[:], T.loc[:, W - 1:W + 1], sem.arr, sem.sent, pid, rid, m)
+    else:
+        g.vector.wait_ge(sem.lx, 16)
+
+    if r == 0:
+        g.vector.tensor_tensor_scan(T.y_sb[:], T.gate[:], T.x_sb[:], 0.0, mult, add).then_inc(sem.sy, 1)
+    else:
+        g.sync.wait_ge(sem.arr, r)
+        g.sync.dma_start(T.rows[0:r, :], T.land[0:r]).then_inc(sem.lr, 16)
+        g.tensor.wait_ge(sem.idn, 1)
+        g.tensor.wait_ge(sem.lr, 16)
+        g.tensor.matmul(T.ps_s[:, 0:r], T.rows[0:r, 0:256:2], T.ident[0:r, 0:r], True, True).then_inc(sem.m1, 1)
+        g.tensor.matmul(T.ps_p[:, 0:r], T.rows[0:r, 1:256:2], T.ident[0:r, 0:r], True, True).then_inc(sem.m2, 1)
+        g.vector.wait_ge(sem.m1, 1)
+        g.vector.tensor_copy(T.s_sb[:, 0:r], T.ps_s[:, 0:r]).then_inc(sem.cp, 1)
+        g.vector.wait_ge(sem.m2, 1)
+        g.vector.wait_ge(sem.cp, 1)
+        g.vector.tensor_tensor_scan(T.car[:, 0:r], T.ps_p[:, 0:r], T.s_sb[:, 0:r], 0.0, mult, add).then_inc(sem.cc, 1)
+        g.vector.wait_ge(sem.cc, 1)
+        g.vector.tensor_tensor_scan(T.y_sb[:], T.gate[:], T.x_sb[:], T.car[:, r - 1:r], mult, add).then_inc(sem.sy, 1)
+
+    g.sync.wait_ge(sem.sy, 1)
+    g.sync.dma_start(T.y[:], T.y_sb[:]).then_inc(sem.st, 16)
+    g.sync.wait_ge(sem.st, 16)
+    if r < N - 1:
+        g.wait_ge(sem.sent, HOP1_ENGINES)

@@ -4,114 +4,118 @@ from concourse.mybir import AluOpType, AxisListType, ActivationFunctionType
 N = 10
 W = 64
 SIM_CORES = 256
-HOP1_ENGINES = 8
-DESTS_PER_ENGINE = 3
+E_CHIP = 8
+E_PASS = 8
+E_SELF = 8
+ROOM = (3, 2)
+OWN = 3
+HEAD = 96
+B = 2 * N
+Z = B + 2 * W
 
 SCRATCH = {
     "a_sb": ("sbuf", [128, W], "bfloat16"),
     "x_sb": ("sbuf", [128, W], "bfloat16"),
-    "gate": ("sbuf", [128, W], "float32"),
+    "z": ("sbuf", [128, Z], "float32"),
     "loc": ("sbuf", [128, W + 1], "float32"),
-    "stage": ("dram", [128, 2], "float32"),
-    "land": ("dram", [N - 1, 128, 2], "float32"),
-    "rows": ("sbuf", [128, 256], "float32"),
-    "ones": ("sbuf", [128, N - 1], "float32"),
-    "ident": ("sbuf", [128, N - 1], "float32"),
-    "ps_s": ("psum", [128, 512], "float32"),
-    "ps_p": ("psum", [128, 512], "float32"),
-    "s_sb": ("sbuf", [128, N - 1], "float32"),
-    "car": ("sbuf", [128, N - 1], "float32"),
-    "y_sb": ("sbuf", [128, W], "bfloat16"),
+    "h_sb": ("sbuf", [128, N + W], "bfloat16"),
 }
-SEMAPHORES = ["la", "lx", "on", "idn", "sg", "sv", "arr", "sent", "lr", "m1", "m2", "cp", "cc", "sy", "st"]
+SEMAPHORES = ["la0", "la1", "lx", "sg", "sv", "xc", "arr", "sent", "sy", "st"]
 
 
 def _bits(mask):
     return [1 << b for b in range(mask.bit_length()) if (mask >> b) & 1]
 
 
-def _port_owner(c, dests, topo):
+def _plan(j, T, topo):
+    c = T.cores[j]
+    later = list(T.cores[j + 1:])
+    direct = [k for k in later if topo.may_write(c, k)]
+    cross = [k for k in later if not topo.may_write(c, k)]
     ok = [d for d in range(SIM_CORES)
           if d != c and topo.host(d) == topo.host(c) and topo.chip(d) == topo.chip(c)
-          and all(topo.may_write(d, k) for k in dests)]
+          and all(topo.may_write(d, k) for k in later)]
     same = [d for d in ok if topo.die(d) == topo.die(c)]
-    return (same or ok)[0]
+    helpers = (same + [d for d in ok if d not in same])[:min(len(ROOM), len(cross))]
+    shares = {}
+    for i, d in enumerate(helpers):
+        shares[d] = cross[i::len(helpers)]
+    for i, d in enumerate(helpers):
+        while len(shares[d]) < ROOM[i] and len(direct) > OWN:
+            shares[d].append(direct.pop())
+    return direct, shares
 
 
-def _relay_program(g, core, j, T, topo):
-    sem = T.sem
-    dests = list(T.cores[j + 1:])
+def _slot(j, d, T):
+    k = T.rank_of(d)
+    q = 0 if k is None else N - k + j
+    return T.z[:, 2 * q:2 * q + 2]
+
+
+def _send(g, core, j, src, dests, engines, T, topo):
     common = topo.mask(core, dests[0])
+    ids = []
     for d in dests:
         common &= topo.mask(core, d)
-    engines = _bits(common)[0::2]
-    transfers = []
-    for i in range(0, len(dests), DESTS_PER_ENGINE):
-        part = dests[i:i + DESTS_PER_ENGINE]
-        ids = []
-        for d in part:
-            rid, pid = topo.addr(d, core)
-            ids.append(DstId(rid=rid, pnc=pid))
-        transfers.append(RemoteDMATransfer(dst_ids=ids, dma_engine_mask=engines[len(transfers)], remote_sem=sem.arr,
-                                           srcs=[T.stage[:]], dsts=[T.land[j] for _ in part]))
-    g.wait_ge(sem.arr, HOP1_ENGINES)
-    g.remote_dma_fused(transfers, local_sem=sem.sent)
-    g.wait_ge(sem.sent, len(transfers))
+        rid, pid = topo.addr(d, core)
+        ids.append(DstId(rid=rid, pnc=pid))
+    g.remote_dma_fused([RemoteDMATransfer(dst_ids=ids, dma_engine_mask=sum(_bits(common)[:engines]),
+                                          remote_sem=T.sem.arr, srcs=[src],
+                                          dsts=[_slot(j, d, T) for d in dests])], local_sem=T.sem.sent)
 
 
 def rank_program(g, core, T, topo):
     sem = T.sem
     mult, add = AluOpType.mult, AluOpType.add
+    sigmoid = ActivationFunctionType.Sigmoid
     r = T.rank_of(core)
     if r is None:
         for j in range(N - 1):
-            if _port_owner(T.cores[j], T.cores[j + 1:], topo) == core:
-                _relay_program(g, core, j, T, topo)
+            shares = _plan(j, T, topo)[1]
+            if core in shares:
+                g.wait_ge(sem.arr, E_CHIP)
+                _send(g, core, j, _slot(j, core, T), shares[core], E_PASS, T, topo)
+                g.wait_ge(sem.sent, E_PASS)
         return
 
-    g.sync.dma_start(T.a_sb[:], T.a[:]).then_inc(sem.la, 16)
+    gate = T.z[:, B + 1:Z:2]
+
+    g.sync.dma_start(T.a_sb[HEAD:128, :], T.a[HEAD:128, :]).then_inc(sem.la0, 16)
+    g.sync.dma_start(T.a_sb[0:HEAD, :], T.a[0:HEAD, :]).then_inc(sem.la1, 16)
     g.sync.dma_start(T.x_sb[:], T.x[:]).then_inc(sem.lx, 16)
 
-    if r > 0:
-        g.vector.memset(T.ones[0:r, 0:r], 1.0).then_inc(sem.on, 1)
-        g.wait_ge(sem.on, 1)
-        g.affine_select(T.ident[0:r, 0:r], T.ones[0:r, 0:r], [[-1, r]], AluOpType.is_equal, 0.0, 0, 1).then_inc(sem.idn, 1)
+    g.scalar.wait_ge(sem.la0, 16)
+    g.scalar.activation(T.z[HEAD:128, B + 1:Z:2], T.a_sb[HEAD:128, :], sigmoid).then_inc(sem.sg, 1)
+    g.scalar.wait_ge(sem.la1, 16)
+    g.scalar.activation(T.z[0:HEAD, B + 1:Z:2], T.a_sb[0:HEAD, :], sigmoid).then_inc(sem.sg, 1)
 
-    g.scalar.wait_ge(sem.la, 16)
-    g.scalar.activation(T.gate[:], T.a_sb[:], ActivationFunctionType.Sigmoid).then_inc(sem.sg, 1)
-
-    g.vector.wait_ge(sem.sg, 1)
+    g.vector.wait_ge(sem.sg, 2)
+    left = 0
     if r < N - 1:
-        g.vector.tensor_reduce(T.loc[:, W:W + 1], T.gate[:], AxisListType.X, mult).then_inc(sem.sv, 1)
+        g.vector.tensor_reduce(T.loc[:, W:W + 1], gate, AxisListType.X, mult).then_inc(sem.sv, 1)
         g.vector.wait_ge(sem.lx, 16)
-        g.vector.tensor_tensor_scan(T.loc[:, 0:W], T.gate[:], T.x_sb[:], 0.0, mult, add).then_inc(sem.sv, 1)
-        relay = _port_owner(core, T.cores[r + 1:], topo)
-        rid, pid = topo.addr(relay, core)
-        m = sum(_bits(topo.mask(core, relay))[:HOP1_ENGINES])
+        g.vector.tensor_tensor_scan(T.loc[:, 0:W], gate, T.x_sb[:], 0.0, mult, add).then_inc(sem.sv, 1)
+        direct, shares = _plan(r, T, topo)
         g.wait_ge(sem.sv, 2)
-        g.remote_dma(T.stage[:], T.loc[:, W - 1:W + 1], sem.arr, sem.sent, pid, rid, m)
+        for dests, engines in ((list(shares), E_CHIP), (direct, E_SELF)):
+            if dests:
+                _send(g, core, r, T.loc[:, W - 1:W + 1], dests, engines, T, topo)
+                left += engines
     else:
         g.vector.wait_ge(sem.lx, 16)
 
     if r == 0:
-        g.vector.tensor_tensor_scan(T.y_sb[:], T.gate[:], T.x_sb[:], 0.0, mult, add).then_inc(sem.sy, 1)
+        g.vector.tensor_tensor_scan(T.h_sb[:, 0:W], gate, T.x_sb[:], 0.0, mult, add).then_inc(sem.sy, 1)
     else:
-        g.sync.wait_ge(sem.arr, r)
-        g.sync.dma_start(T.rows[0:r, :], T.land[0:r]).then_inc(sem.lr, 16)
-        g.tensor.wait_ge(sem.idn, 1)
-        g.tensor.wait_ge(sem.lr, 16)
-        g.tensor.matmul(T.ps_s[:, 0:r], T.rows[0:r, 0:256:2], T.ident[0:r, 0:r], True, True).then_inc(sem.m1, 1)
-        g.tensor.matmul(T.ps_p[:, 0:r], T.rows[0:r, 1:256:2], T.ident[0:r, 0:r], True, True).then_inc(sem.m2, 1)
-        g.vector.wait_ge(sem.m1, 1)
-        g.vector.tensor_copy(T.s_sb[:, 0:r], T.ps_s[:, 0:r]).then_inc(sem.cp, 1)
-        g.vector.wait_ge(sem.m2, 1)
-        g.vector.wait_ge(sem.cp, 1)
-        g.vector.tensor_tensor_scan(T.car[:, 0:r], T.ps_p[:, 0:r], T.s_sb[:, 0:r], 0.0, mult, add).then_inc(sem.cc, 1)
-        g.vector.wait_ge(sem.cc, 1)
-        g.vector.tensor_tensor_scan(T.y_sb[:], T.gate[:], T.x_sb[:], T.car[:, r - 1:r], mult, add).then_inc(sem.sy, 1)
+        g.vector.tensor_copy(T.z[:, B:Z:2], T.x_sb[:]).then_inc(sem.xc, 1)
+        g.vector.wait_ge(sem.xc, 1)
+        due = sum(E_SELF if core in _plan(j, T, topo)[0] else E_PASS for j in range(r))
+        g.vector.wait_ge(sem.arr, due)
+        f = B - 2 * r
+        g.vector.tensor_tensor_scan(T.h_sb[:, 0:r + W], T.z[:, f + 1:Z:2], T.z[:, f:Z:2], 0.0, mult, add).then_inc(sem.sy, 1)
 
     g.sync.wait_ge(sem.sy, 1)
-    g.sync.dma_start(T.y[:], T.y_sb[:]).then_inc(sem.st, 16)
+    g.sync.dma_start(T.y[:], T.h_sb[:, r:r + W]).then_inc(sem.st, 16)
     g.sync.wait_ge(sem.st, 16)
-    if r < N - 1:
-        g.wait_ge(sem.sent, HOP1_ENGINES)
+    if left:
+        g.wait_ge(sem.sent, left)

@@ -10,17 +10,17 @@ E_SELF = 8
 ROOM = (3, 2)
 OWN = 3
 HEAD = 96
-B = 2 * N
+B = 4 * N
 Z = B + 2 * W
 
 SCRATCH = {
     "a_sb": ("sbuf", [128, W], "bfloat16"),
     "x_sb": ("sbuf", [128, W], "bfloat16"),
-    "z": ("sbuf", [128, Z], "float32"),
-    "loc": ("sbuf", [128, W + 1], "float32"),
-    "h_sb": ("sbuf", [128, N + W], "bfloat16"),
+    "z": ("sbuf", [128, Z + 4], "float32"),
+    "sc": ("sbuf", [128, W + 4], "float32"),
+    "h_sb": ("sbuf", [128, 2 * N + W], "bfloat16"),
 }
-SEMAPHORES = ["la0", "la1", "lx", "sg", "sv", "xc", "arr", "sent", "sy", "st"]
+SEMAPHORES = ["la0", "la1", "lx", "sg", "se", "sv", "xc", "arre", "arr", "sent", "sy", "st"]
 
 
 def _bits(mask):
@@ -46,13 +46,13 @@ def _plan(j, T, topo):
     return direct, shares
 
 
-def _slot(j, d, T):
+def _slot(j, d, T, lo, hi):
     k = T.rank_of(d)
     q = 0 if k is None else N - k + j
-    return T.z[:, 2 * q:2 * q + 2]
+    return T.z[:, 4 * q + lo:4 * q + hi]
 
 
-def _send(g, core, j, src, dests, engines, T, topo):
+def _send(g, core, j, src, dests, lo, hi, engines, rsem, T, topo):
     common = topo.mask(core, dests[0])
     ids = []
     for d in dests:
@@ -60,8 +60,9 @@ def _send(g, core, j, src, dests, engines, T, topo):
         rid, pid = topo.addr(d, core)
         ids.append(DstId(rid=rid, pnc=pid))
     g.remote_dma_fused([RemoteDMATransfer(dst_ids=ids, dma_engine_mask=sum(_bits(common)[:engines]),
-                                          remote_sem=T.sem.arr, srcs=[src],
-                                          dsts=[_slot(j, d, T) for d in dests])], local_sem=T.sem.sent)
+                                          remote_sem=rsem, srcs=[src],
+                                          dsts=[_slot(j, d, T, lo, hi) for d in dests])], local_sem=T.sem.sent)
+    return engines
 
 
 def rank_program(g, core, T, topo):
@@ -73,49 +74,77 @@ def rank_program(g, core, T, topo):
         for j in range(N - 1):
             shares = _plan(j, T, topo)[1]
             if core in shares:
+                mine = shares[core]
+                g.wait_ge(sem.arre, E_CHIP)
+                left = _send(g, core, j, _slot(j, core, T, 2, 4), mine[:1], 2, 4, E_PASS, sem.arr, T, topo)
                 g.wait_ge(sem.arr, E_CHIP)
-                _send(g, core, j, _slot(j, core, T), shares[core], E_PASS, T, topo)
-                g.wait_ge(sem.sent, E_PASS)
+                if mine[1:]:
+                    left += _send(g, core, j, _slot(j, core, T, 0, 4), mine[1:], 0, 4, E_PASS, sem.arr, T, topo)
+                left += _send(g, core, j, _slot(j, core, T, 0, 2), mine[:1], 0, 2, E_PASS, sem.arr, T, topo)
+                g.wait_ge(sem.sent, left)
         return
 
-    gate = T.z[:, B + 1:Z:2]
+    sends = r < N - 1
 
     g.sync.dma_start(T.a_sb[HEAD:128, :], T.a[HEAD:128, :]).then_inc(sem.la0, 16)
-    g.sync.dma_start(T.a_sb[0:HEAD, :], T.a[0:HEAD, :]).then_inc(sem.la1, 16)
     g.sync.dma_start(T.x_sb[:], T.x[:]).then_inc(sem.lx, 16)
+    g.sync.dma_start(T.a_sb[0:HEAD, :], T.a[0:HEAD, :]).then_inc(sem.la1, 16)
 
     g.scalar.wait_ge(sem.la0, 16)
     g.scalar.activation(T.z[HEAD:128, B + 1:Z:2], T.a_sb[HEAD:128, :], sigmoid).then_inc(sem.sg, 1)
     g.scalar.wait_ge(sem.la1, 16)
     g.scalar.activation(T.z[0:HEAD, B + 1:Z:2], T.a_sb[0:HEAD, :], sigmoid).then_inc(sem.sg, 1)
 
-    g.vector.wait_ge(sem.sg, 2)
-    left = 0
-    if r < N - 1:
-        g.vector.tensor_reduce(T.loc[:, W:W + 1], gate, AxisListType.X, mult).then_inc(sem.sv, 1)
+    ready = 1
+    if sends:
+        g.vector.memset(T.sc[:, W + 3:W + 4], 1.0).then_inc(sem.se, 1)
+        g.vector.memset(T.z[:, Z + 1:Z + 2], 1.0).then_inc(sem.xc, 1)
         g.vector.wait_ge(sem.lx, 16)
-        g.vector.tensor_tensor_scan(T.loc[:, 0:W], gate, T.x_sb[:], 0.0, mult, add).then_inc(sem.sv, 1)
-        direct, shares = _plan(r, T, topo)
-        g.wait_ge(sem.sv, 2)
-        for dests, engines in ((list(shares), E_CHIP), (direct, E_SELF)):
-            if dests:
-                _send(g, core, r, T.loc[:, W - 1:W + 1], dests, engines, T, topo)
-                left += engines
+        g.vector.tensor_reduce(T.sc[:, W + 2:W + 3], T.x_sb[:], AxisListType.X, add).then_inc(sem.se, 1)
+        g.vector.tensor_reduce(T.z[:, Z:Z + 1], T.x_sb[:], AxisListType.X, add, negate=True).then_inc(sem.xc, 1)
+        ready = 3
     else:
         g.vector.wait_ge(sem.lx, 16)
+    g.vector.tensor_copy(T.z[:, B:Z:2], T.x_sb[:]).then_inc(sem.xc, 1)
+
+    left = 0
+    if sends:
+        direct, shares = _plan(r, T, topo)
+        g.wait_ge(sem.se, 2)
+        left += _send(g, core, r, T.sc[:, W + 2:W + 4], list(shares), 2, 4, E_CHIP, sem.arre, T, topo)
+
+    g.vector.wait_ge(sem.sg, 2)
+    if sends:
+        g.vector.tensor_reduce(T.sc[:, W + 1:W + 2], T.z[:, B + 1:Z:2], AxisListType.X, mult).then_inc(sem.sv, 1)
+        g.vector.wait_ge(sem.xc, ready)
+        g.vector.tensor_tensor_scan(T.sc[:, 0:W + 1], T.z[:, B + 1:Z + 2:2], T.z[:, B:Z + 2:2], 0.0,
+                                    mult, add).then_inc(sem.sv, 1)
+        g.wait_ge(sem.sv, 2)
+        left += _send(g, core, r, T.sc[:, W:W + 2], list(shares), 0, 2, E_CHIP, sem.arr, T, topo)
+        if direct:
+            left += _send(g, core, r, T.sc[:, W:W + 4], direct, 0, 4, E_SELF, sem.arr, T, topo)
+    else:
+        g.vector.wait_ge(sem.xc, ready)
 
     if r == 0:
-        g.vector.tensor_tensor_scan(T.h_sb[:, 0:W], gate, T.x_sb[:], 0.0, mult, add).then_inc(sem.sy, 1)
+        g.vector.tensor_tensor_scan(T.h_sb[:, 0:W], T.z[:, B + 1:Z:2], T.x_sb[:], 0.0, mult, add).then_inc(sem.sy, 1)
     else:
-        g.vector.tensor_copy(T.z[:, B:Z:2], T.x_sb[:]).then_inc(sem.xc, 1)
-        g.vector.wait_ge(sem.xc, 1)
-        due = sum(E_SELF if core in _plan(j, T, topo)[0] else E_PASS for j in range(r))
+        due = 0
+        for j in range(r):
+            direct_j, shares_j = _plan(j, T, topo)
+            if core in direct_j:
+                due += E_SELF
+            else:
+                for mine in shares_j.values():
+                    if core in mine:
+                        due += 2 * E_PASS if mine[0] == core else E_PASS
         g.vector.wait_ge(sem.arr, due)
-        f = B - 2 * r
-        g.vector.tensor_tensor_scan(T.h_sb[:, 0:r + W], T.z[:, f + 1:Z:2], T.z[:, f:Z:2], 0.0, mult, add).then_inc(sem.sy, 1)
+        f = B - 4 * r
+        g.vector.tensor_tensor_scan(T.h_sb[:, 0:2 * r + W], T.z[:, f + 1:Z:2], T.z[:, f:Z:2], 0.0,
+                                    mult, add).then_inc(sem.sy, 1)
 
     g.sync.wait_ge(sem.sy, 1)
-    g.sync.dma_start(T.y[:], T.h_sb[:, r:r + W]).then_inc(sem.st, 16)
+    g.sync.dma_start(T.y[:], T.h_sb[:, 2 * r:2 * r + W]).then_inc(sem.st, 16)
     g.sync.wait_ge(sem.st, 16)
     if left:
         g.wait_ge(sem.sent, left)

@@ -9,18 +9,18 @@ E_PASS = 8
 E_SELF = 8
 ROOM = (3, 2)
 OWN = 3
-HEAD = 96
+BIG = 64.0
 B = 4 * N
 Z = B + 2 * W
 
 SCRATCH = {
-    "a_sb": ("sbuf", [128, W], "bfloat16"),
+    "a_sb": ("sbuf", [128, W + 8], "bfloat16"),
     "x_sb": ("sbuf", [128, W], "bfloat16"),
     "z": ("sbuf", [128, Z + 4], "float32"),
     "sc": ("sbuf", [128, W + 4], "float32"),
     "h_sb": ("sbuf", [128, 2 * N + W], "bfloat16"),
 }
-SEMAPHORES = ["la0", "la1", "lx", "sg", "se", "sv", "xc", "arre", "arr", "sent", "sy", "st"]
+SEMAPHORES = ["la", "lx", "k0", "k1", "sg", "se", "sv", "xc", "arre", "arr", "sent", "sy", "st"]
 
 
 def _bits(mask):
@@ -72,57 +72,68 @@ def rank_program(g, core, T, topo):
     r = T.rank_of(core)
     if r is None:
         for j in range(N - 1):
-            shares = _plan(j, T, topo)[1]
+            direct, shares = _plan(j, T, topo)
             if core in shares:
                 mine = shares[core]
-                g.wait_ge(sem.arre, E_CHIP)
-                left = _send(g, core, j, _slot(j, core, T, 2, 4), mine[:1], 2, 4, E_PASS, sem.arr, T, topo)
+                g.vector.memset(T.sc[:, 0:4], 1.0).then_inc(sem.k1, 1)
+                g.wait_ge(sem.k1, 1)
+                left = _send(g, core, j, T.sc[:, 0:1], mine[:1], 3, 4, E_PASS, sem.arr, T, topo)
+                if not direct:
+                    g.wait_ge(sem.arre, E_CHIP)
                 g.wait_ge(sem.arr, E_CHIP)
                 if mine[1:]:
                     left += _send(g, core, j, _slot(j, core, T, 0, 4), mine[1:], 0, 4, E_PASS, sem.arr, T, topo)
-                left += _send(g, core, j, _slot(j, core, T, 0, 2), mine[:1], 0, 2, E_PASS, sem.arr, T, topo)
+                left += _send(g, core, j, _slot(j, core, T, 0, 3), mine[:1], 0, 3, E_PASS, sem.arr, T, topo)
                 g.wait_ge(sem.sent, left)
         return
 
     sends = r < N - 1
+    direct, shares = _plan(r, T, topo) if sends else ([], {})
 
-    g.sync.dma_start(T.a_sb[HEAD:128, :], T.a[HEAD:128, :]).then_inc(sem.la0, 16)
-    g.sync.dma_start(T.x_sb[:], T.x[:]).then_inc(sem.lx, 16)
-    g.sync.dma_start(T.a_sb[0:HEAD, :], T.a[0:HEAD, :]).then_inc(sem.la1, 16)
+    g.sync.dma_start(T.a_sb[:, 0:W], T.a[:]).then_inc(sem.la, 16)
+    g.scalar.dma_start(T.x_sb[:], T.x[:]).then_inc(sem.lx, 16)
 
-    g.scalar.wait_ge(sem.la0, 16)
-    g.scalar.activation(T.z[HEAD:128, B + 1:Z:2], T.a_sb[HEAD:128, :], sigmoid).then_inc(sem.sg, 1)
-    g.scalar.wait_ge(sem.la1, 16)
-    g.scalar.activation(T.z[0:HEAD, B + 1:Z:2], T.a_sb[0:HEAD, :], sigmoid).then_inc(sem.sg, 1)
+    gates = 1
+    if sends:
+        g.vector.memset(T.a_sb[:, W:W + 8], BIG).then_inc(sem.k0, 1)
+        g.scalar.wait_ge(sem.k0, 1)
+        g.scalar.activation(T.z[:, Z + 1:Z + 2], T.a_sb[:, W:W + 1], sigmoid).then_inc(sem.sg, 1)
+        gates = 2
+    g.scalar.wait_ge(sem.la, 16)
+    g.scalar.activation(T.z[:, B + 1:Z:2], T.a_sb[:, 0:W], sigmoid).then_inc(sem.sg, 1)
 
+    left = 0
     ready = 1
     if sends:
-        g.vector.memset(T.sc[:, W + 3:W + 4], 1.0).then_inc(sem.se, 1)
-        g.vector.memset(T.z[:, Z + 1:Z + 2], 1.0).then_inc(sem.xc, 1)
+        if direct:
+            g.vector.memset(T.sc[:, W + 3:W + 4], 1.0).then_inc(sem.k1, 1)
+            g.wait_ge(sem.k1, 1)
+            left += _send(g, core, r, T.sc[:, W + 3:W + 4], direct[:1], 3, 4, E_SELF, sem.arr, T, topo)
         g.vector.wait_ge(sem.lx, 16)
         g.vector.tensor_reduce(T.sc[:, W + 2:W + 3], T.x_sb[:], AxisListType.X, add).then_inc(sem.se, 1)
         g.vector.tensor_reduce(T.z[:, Z:Z + 1], T.x_sb[:], AxisListType.X, add, negate=True).then_inc(sem.xc, 1)
-        ready = 3
+        ready = 2
+        g.wait_ge(sem.se, 1)
+        if not direct:
+            left += _send(g, core, r, T.sc[:, W + 2:W + 3], list(shares), 2, 3, E_CHIP, sem.arre, T, topo)
     else:
         g.vector.wait_ge(sem.lx, 16)
     g.vector.tensor_copy(T.z[:, B:Z:2], T.x_sb[:]).then_inc(sem.xc, 1)
 
-    left = 0
-    if sends:
-        direct, shares = _plan(r, T, topo)
-        g.wait_ge(sem.se, 2)
-        left += _send(g, core, r, T.sc[:, W + 2:W + 4], list(shares), 2, 4, E_CHIP, sem.arre, T, topo)
-
-    g.vector.wait_ge(sem.sg, 2)
+    g.vector.wait_ge(sem.sg, gates)
     if sends:
         g.vector.tensor_reduce(T.sc[:, W + 1:W + 2], T.z[:, B + 1:Z:2], AxisListType.X, mult).then_inc(sem.sv, 1)
         g.vector.wait_ge(sem.xc, ready)
         g.vector.tensor_tensor_scan(T.sc[:, 0:W + 1], T.z[:, B + 1:Z + 2:2], T.z[:, B:Z + 2:2], 0.0,
                                     mult, add).then_inc(sem.sv, 1)
         g.wait_ge(sem.sv, 2)
-        left += _send(g, core, r, T.sc[:, W:W + 2], list(shares), 0, 2, E_CHIP, sem.arr, T, topo)
         if direct:
-            left += _send(g, core, r, T.sc[:, W:W + 4], direct, 0, 4, E_SELF, sem.arr, T, topo)
+            left += _send(g, core, r, T.sc[:, W:W + 4], list(shares), 0, 4, E_CHIP, sem.arr, T, topo)
+            if direct[1:]:
+                left += _send(g, core, r, T.sc[:, W:W + 4], direct[1:], 0, 4, E_SELF, sem.arr, T, topo)
+            left += _send(g, core, r, T.sc[:, W:W + 3], direct[:1], 0, 3, E_SELF, sem.arr, T, topo)
+        else:
+            left += _send(g, core, r, T.sc[:, W:W + 2], list(shares), 0, 2, E_CHIP, sem.arr, T, topo)
     else:
         g.vector.wait_ge(sem.xc, ready)
 
@@ -133,7 +144,7 @@ def rank_program(g, core, T, topo):
         for j in range(r):
             direct_j, shares_j = _plan(j, T, topo)
             if core in direct_j:
-                due += E_SELF
+                due += 2 * E_SELF if direct_j[0] == core else E_SELF
             else:
                 for mine in shares_j.values():
                     if core in mine:

from concourse.bass import DstId, RemoteDMATransfer
from concourse.mybir import AluOpType, AxisListType, ActivationFunctionType

N = 10
W = 64
SIM_CORES = 256
E_CHIP = 8
E_PASS = 8
E_SELF = 8
ROOM = (3, 2)
OWN = 3
BIG = 64.0
B = 4 * N
Z = B + 2 * W

SCRATCH = {
    "a_sb": ("sbuf", [128, W + 8], "bfloat16"),
    "x_sb": ("sbuf", [128, W], "bfloat16"),
    "z": ("sbuf", [128, Z + 4], "float32"),
    "sc": ("sbuf", [128, W + 4], "float32"),
    "h_sb": ("sbuf", [128, 2 * N + W], "bfloat16"),
}
SEMAPHORES = ["la", "lx", "k0", "k1", "sg", "se", "sv", "xc", "arre", "arr", "sent", "sy", "st"]


def _bits(mask):
    return [1 << b for b in range(mask.bit_length()) if (mask >> b) & 1]


def _plan(j, T, topo):
    c = T.cores[j]
    later = list(T.cores[j + 1:])
    direct = [k for k in later if topo.may_write(c, k)]
    cross = [k for k in later if not topo.may_write(c, k)]
    ok = [d for d in range(SIM_CORES)
          if d != c and topo.host(d) == topo.host(c) and topo.chip(d) == topo.chip(c)
          and all(topo.may_write(d, k) for k in later)]
    same = [d for d in ok if topo.die(d) == topo.die(c)]
    helpers = (same + [d for d in ok if d not in same])[:min(len(ROOM), len(cross))]
    shares = {}
    for i, d in enumerate(helpers):
        shares[d] = cross[i::len(helpers)]
    for i, d in enumerate(helpers):
        while len(shares[d]) < ROOM[i] and len(direct) > OWN:
            shares[d].append(direct.pop())
    return direct, shares


def _slot(j, d, T, lo, hi):
    k = T.rank_of(d)
    q = 0 if k is None else N - k + j
    return T.z[:, 4 * q + lo:4 * q + hi]


def _send(g, core, j, src, dests, lo, hi, engines, rsem, T, topo):
    common = topo.mask(core, dests[0])
    ids = []
    for d in dests:
        common &= topo.mask(core, d)
        rid, pid = topo.addr(d, core)
        ids.append(DstId(rid=rid, pnc=pid))
    g.remote_dma_fused([RemoteDMATransfer(dst_ids=ids, dma_engine_mask=sum(_bits(common)[:engines]),
                                          remote_sem=rsem, srcs=[src],
                                          dsts=[_slot(j, d, T, lo, hi) for d in dests])], local_sem=T.sem.sent)
    return engines


def rank_program(g, core, T, topo):
    sem = T.sem
    mult, add = AluOpType.mult, AluOpType.add
    sigmoid = ActivationFunctionType.Sigmoid
    r = T.rank_of(core)
    if r is None:
        for j in range(N - 1):
            direct, shares = _plan(j, T, topo)
            if core in shares:
                mine = shares[core]
                g.vector.memset(T.sc[:, 0:4], 1.0).then_inc(sem.k1, 1)
                g.wait_ge(sem.k1, 1)
                left = _send(g, core, j, T.sc[:, 0:1], mine[:1], 3, 4, E_PASS, sem.arr, T, topo)
                if not direct:
                    g.wait_ge(sem.arre, E_CHIP)
                g.wait_ge(sem.arr, E_CHIP)
                if mine[1:]:
                    left += _send(g, core, j, _slot(j, core, T, 0, 4), mine[1:], 0, 4, E_PASS, sem.arr, T, topo)
                left += _send(g, core, j, _slot(j, core, T, 0, 3), mine[:1], 0, 3, E_PASS, sem.arr, T, topo)
                g.wait_ge(sem.sent, left)
        return

    sends = r < N - 1
    direct, shares = _plan(r, T, topo) if sends else ([], {})

    g.sync.dma_start(T.a_sb[:, 0:W], T.a[:]).then_inc(sem.la, 16)
    g.scalar.dma_start(T.x_sb[:], T.x[:]).then_inc(sem.lx, 16)

    gates = 1
    if sends:
        g.vector.memset(T.a_sb[:, W:W + 8], BIG).then_inc(sem.k0, 1)
        g.scalar.wait_ge(sem.k0, 1)
        g.scalar.activation(T.z[:, Z + 1:Z + 2], T.a_sb[:, W:W + 1], sigmoid).then_inc(sem.sg, 1)
        gates = 2
    g.scalar.wait_ge(sem.la, 16)
    g.scalar.activation(T.z[:, B + 1:Z:2], T.a_sb[:, 0:W], sigmoid).then_inc(sem.sg, 1)

    left = 0
    ready = 1
    if sends:
        if direct:
            g.vector.memset(T.sc[:, W + 3:W + 4], 1.0).then_inc(sem.k1, 1)
            g.wait_ge(sem.k1, 1)
            left += _send(g, core, r, T.sc[:, W + 3:W + 4], direct[:1], 3, 4, E_SELF, sem.arr, T, topo)
        g.vector.wait_ge(sem.lx, 16)
        g.vector.tensor_reduce(T.sc[:, W + 2:W + 3], T.x_sb[:], AxisListType.X, add).then_inc(sem.se, 1)
        g.vector.tensor_reduce(T.z[:, Z:Z + 1], T.x_sb[:], AxisListType.X, add, negate=True).then_inc(sem.xc, 1)
        ready = 2
        g.wait_ge(sem.se, 1)
        if not direct:
            left += _send(g, core, r, T.sc[:, W + 2:W + 3], list(shares), 2, 3, E_CHIP, sem.arre, T, topo)
    else:
        g.vector.wait_ge(sem.lx, 16)
    g.vector.tensor_copy(T.z[:, B:Z:2], T.x_sb[:]).then_inc(sem.xc, 1)

    g.vector.wait_ge(sem.sg, gates)
    if sends:
        g.vector.tensor_reduce(T.sc[:, W + 1:W + 2], T.z[:, B + 1:Z:2], AxisListType.X, mult).then_inc(sem.sv, 1)
        g.vector.wait_ge(sem.xc, ready)
        g.vector.tensor_tensor_scan(T.sc[:, 0:W + 1], T.z[:, B + 1:Z + 2:2], T.z[:, B:Z + 2:2], 0.0,
                                    mult, add).then_inc(sem.sv, 1)
        g.wait_ge(sem.sv, 2)
        if direct:
            left += _send(g, core, r, T.sc[:, W:W + 4], list(shares), 0, 4, E_CHIP, sem.arr, T, topo)
            if direct[1:]:
                left += _send(g, core, r, T.sc[:, W:W + 4], direct[1:], 0, 4, E_SELF, sem.arr, T, topo)
            left += _send(g, core, r, T.sc[:, W:W + 3], direct[:1], 0, 3, E_SELF, sem.arr, T, topo)
        else:
            left += _send(g, core, r, T.sc[:, W:W + 2], list(shares), 0, 2, E_CHIP, sem.arr, T, topo)
    else:
        g.vector.wait_ge(sem.xc, ready)

    if r == 0:
        g.vector.tensor_tensor_scan(T.h_sb[:, 0:W], T.z[:, B + 1:Z:2], T.x_sb[:], 0.0, mult, add).then_inc(sem.sy, 1)
    else:
        due = 0
        for j in range(r):
            direct_j, shares_j = _plan(j, T, topo)
            if core in direct_j:
                due += 2 * E_SELF if direct_j[0] == core else E_SELF
            else:
                for mine in shares_j.values():
                    if core in mine:
                        due += 2 * E_PASS if mine[0] == core else E_PASS
        g.vector.wait_ge(sem.arr, due)
        f = B - 4 * r
        g.vector.tensor_tensor_scan(T.h_sb[:, 0:2 * r + W], T.z[:, f + 1:Z:2], T.z[:, f:Z:2], 0.0,
                                    mult, add).then_inc(sem.sy, 1)

    g.sync.wait_ge(sem.sy, 1)
    g.sync.dma_start(T.y[:], T.h_sb[:, 2 * r:2 * r + W]).then_inc(sem.st, 16)
    g.sync.wait_ge(sem.st, 16)
    if left:
        g.wait_ge(sem.sent, left)
